import numpy as np
import ml_dtypes


def mxq(x, axis, fmt="e4m3"):
    dtype, down = {"e4m3": (ml_dtypes.float8_e4m3fn, 7), "e5m2": (ml_dtypes.float8_e5m2, 14)}[fmt]
    v = np.moveaxis(np.asarray(x, np.float32).astype(ml_dtypes.bfloat16).astype(np.float64), axis, -1)
    blocks = v.reshape(v.shape[:-1] + (-1, 32))
    amax = np.abs(blocks).max(-1, keepdims=True)
    byte = np.maximum(np.where(amax > 0, np.frexp(amax)[1] - 1 + 127, 0) - down, 1)
    scale = np.exp2(byte - 127.0)
    codes = (blocks / scale).astype(np.float32).astype(dtype).astype(np.float64)
    return np.moveaxis((codes * scale).reshape(v.shape), -1, axis)


WIDE = False


def mx_kscale(k, group=512):
    if not WIDE:
        return np.ones(k)
    levels = np.array([10, -10, 5, -5, 0])
    if group != 512:
        return np.exp2(np.random.permutation(np.resize(levels, k // group))).repeat(group)
    if k % 512:
        return np.exp2(np.random.permutation(np.resize(levels, k // 32))).repeat(32)
    a = np.empty((k // 512, 16))
    for p in range(k // 512):
        a[p, :8] = np.random.permutation(np.resize(levels, 8))
        for g in range(8):
            far = levels[np.abs(levels - a[p, g]) >= 10]
            a[p, g + 8] = far[np.random.randint(len(far))]
    return np.exp2(a.ravel()).repeat(32)


def f64(x):
    return np.asarray(x).astype(np.float64)


def sigmoid(v):
    return 1.0 / (1.0 + np.exp(-v))


G, D, M, O, N = 2, 256, 128, 256, 512


def setup_inputs():
    n = np.random.standard_normal
    s_d = mx_kscale(D, 0)
    s_o = mx_kscale(O, 0)
    return {
        "x": (n((G, D, N)) * s_d[:, None]).astype(np.float32),
        "w1": (n((G, D, M)) / np.sqrt(D) / s_d[:, None]).astype(np.float32),
        "w2": (n((G, D, M)) / np.sqrt(D) / s_d[:, None]).astype(np.float32),
        "w3": (n((G, D, M)) / np.sqrt(D) / s_d[:, None]).astype(np.float32),
        "wo": (n((G, O, M)) / np.sqrt(O) / s_o[:, None]).astype(np.float32),
        "dy": (n((G, O, N)) * s_o[:, None]).astype(np.float32),
        "dx": (n((G, D, N)) * s_d[:, None]).astype(np.float32),
        "og": (np.random.uniform(0.5, 2.0, (G, M, 1))).astype(np.float32),
        "base": (0.3 * n((G, M, N))).astype(np.float32),
    }


def reference(x, w1, w2, w3, wo, dy, dx, og, base):
    w1q = mxq(f64(w1), 1, "e4m3")
    xq = mxq(f64(x), 1, "e4m3")
    z1 = w1q.transpose(0, 2, 1) @ xq
    dxq = mxq(f64(dx), 1, "e4m3")
    tz1 = w1q.transpose(0, 2, 1) @ dxq
    w2q = mxq(f64(w2), 1, "e4m3")
    z2 = w2q.transpose(0, 2, 1) @ xq
    tz2 = w2q.transpose(0, 2, 1) @ dxq
    w3q = mxq(f64(w3), 1, "e4m3")
    z3 = w3q.transpose(0, 2, 1) @ xq
    tz3 = w3q.transpose(0, 2, 1) @ dxq
    sg = sigmoid(z1 * z2 + z3)
    woq = mxq(f64(wo), 1, "e4m3")
    dyq = mxq(f64(dy), 1, "e4m3")
    c0 = woq.transpose(0, 2, 1) @ dyq
    dsg = c0 * np.tanh(z3)
    xsg = (tz1 * z2 + tz2 * z1 + tz3) * sg * (1.0 - sg)
    xdsg = tz3 * (1.0 - np.square(np.tanh(z3))) * c0
    xdz3 = xsg * c0 * (1.0 - np.square(np.tanh(z3))) + tz3 * (1.0 - np.square(np.tanh(z3))) * np.tanh(z3) * 2.0 * (-1.0) * c0 * sg + (xdsg * sg + xsg * dsg) * (1.0 - sg) + xsg * (-1.0) * dsg * sg
    y = xdz3 * f64(og) + f64(base)
    return y

@@ -1,0 +1,220 @@
+from contextlib import ExitStack
+
+import concourse.mybir as mybir
+
+G, D, M, N = 2, 256, 128, 512
+FLOPS = 7 * 2 * G * D * M * N
+
+F32 = mybir.dt.float32
+BF16 = mybir.dt.bfloat16
+U32 = mybir.dt.uint32
+U8 = mybir.dt.uint8
+FP8X4 = mybir.dt.float8_e4m3fn_x4
+ACT = mybir.ActivationFunctionType
+ALU = mybir.AluOpType
+
+P = 128
+PACK = 4
+ROWS = D // PACK
+HALF = N // 2
+MM_N = 128
+LINE = 4
+
+
+def tile_rows_hvbilinsig_kernel(tc, x, w1, w2, w3, wo, dy, dx, og, base, out):
+    nc = tc.nc
+
+    with ExitStack() as ctx:
+        sb = ctx.enter_context(tc.tile_pool(name="sb", bufs=1))
+        ps = ctx.enter_context(tc.psum_pool(name="ps", bufs=1))
+        ctx.enter_context(tc.manual_schedule())
+
+        raw, packed, codes, scales = {}, {}, {}, {}
+
+        def load(key, src):
+            width = src.shape[2]
+            raw[key] = sb.tile([P, PACK, width], F32, name="raw_" + key)
+            nc.sync.dma_start(out=raw[key][:], in_=src.rearrange("g (p j) c -> (g p) j c", j=PACK))
+
+        def interleave(key, on_vector):
+            width = raw[key].shape[2]
+            packed[key] = sb.tile([P, width, PACK], BF16, name="packed_" + key, align_bytes=64)
+            dst = packed[key][:].rearrange("p (c i) j -> p c j i", i=LINE)
+            src = raw[key][:].rearrange("p j (c i) -> p c j i", i=LINE)
+            if on_vector:
+                nc.vector.tensor_copy(out=dst, in_=src)
+            else:
+                nc.scalar.activation(out=dst, in_=src, func=ACT.Copy)
+
+        def quantize(key):
+            width = raw[key].shape[2]
+            codes[key] = sb.tile([P, width], U32, name="codes_" + key, align_bytes=64)
+            scales[key] = sb.tile([P, width], U8, name="scales_" + key, align_bytes=64)
+            nc.vector.quantize_mx(
+                out=codes[key][:].bitcast(FP8X4),
+                scales=scales[key][:],
+                in_=packed[key][:].rearrange("p c j -> p (c j)"),
+            )
+
+        banks = [[ps.tile([P, 2, HALF], F32, name="bank_%d_%d" % (g, b)) for b in range(4)] for g in range(G)]
+        place = {"z1": (0, 0), "tz1": (0, 1), "z2": (1, 0), "tz2": (1, 1), "z3": (2, 0), "tz3": (3, 0), "c0": (3, 1)}
+
+        def sums(name, g):
+            bank, side = place[name]
+            return banks[g][bank][:, side, :]
+
+        def product(name, weights, columns):
+            for g in range(G):
+                rows = slice(ROWS * g, ROWS * (g + 1))
+                for n0 in range(0, HALF, MM_N):
+                    cols = slice(n0, n0 + MM_N)
+                    nc.tensor.matmul_mx(
+                        out=sums(name, g)[:, cols],
+                        lhsT=codes[weights][rows, :].bitcast(FP8X4),
+                        lhsT_scale=scales[weights][rows, :],
+                        rhs=codes[columns][rows, cols].bitcast(FP8X4),
+                        rhs_scale=scales[columns][rows, cols],
+                        start=True,
+                        stop=True,
+                    )
+
+        vals = {}
+
+        def val(name, h):
+            if (name, h) not in vals:
+                vals[(name, h)] = sb.tile([P, G, HALF], F32, name="%s_%d" % (name, h))
+            return vals[(name, h)]
+
+        def operand(name, h, g):
+            if name in place:
+                return sums(name, g)
+            return val(name, h)[:] if g is None else val(name, h)[:, g, :]
+
+        def act(dst, src, h, g, func, scale=1.0, bias=0.0):
+            nc.scalar.activation(out=operand(dst, h, g), in_=operand(src, h, g), func=func, scale=scale, bias=bias)
+
+        def tt(dst, a, op, b, h, g=None):
+            nc.vector.tensor_tensor(out=operand(dst, h, g), in0=operand(a, h, g), in1=operand(b, h, g), op=op)
+
+        def stt(dst, a, op0, scalar, op1, b, h, g=None):
+            nc.vector.scalar_tensor_tensor(
+                out=operand(dst, h, g), in0=operand(a, h, g), scalar=scalar, in1=operand(b, h, g), op0=op0, op1=op1
+            )
+
+        def half(t, h):
+            return t[:, :, h * HALF : (h + 1) * HALF]
+
+        def load_base(h):
+            nc.sync.dma_start(out=val("base", h)[:], in_=half(base, h).rearrange("g m c -> m g c"))
+
+        load("x0", half(x, 0))
+        load("w1", w1)
+        load("w2", w2)
+        load("w3", w3)
+        load("dx0", half(dx, 0))
+        load("x1", half(x, 1))
+        load("wo", wo)
+        load("dy0", half(dy, 0))
+        gain = sb.tile([P, G, 1], F32, name="gain")
+        with nc.allow_non_contiguous_dma(reason="one gain a partition and group"):
+            nc.sync.dma_start(out=gain[:], in_=og.rearrange("g m o -> m g o"))
+        load("dx1", half(dx, 1))
+        load_base(0)
+        load("dy1", half(dy, 1))
+        load_base(1)
+
+        def forward_products(h):
+            for i in (1, 2, 3):
+                product("z%d" % i, "w%d" % i, "x%d" % h)
+
+        def forward_copies(h):
+            for g in range(G):
+                act("z1s", "z1", h, g, ACT.Copy)
+            for g in range(G):
+                act("T", "z3", h, g, ACT.Tanh)
+
+        def gate_functions(h):
+            act("z2s", "z2", h, 0, ACT.Copy)
+            act("h", "p", h, None, ACT.Tanh, scale=0.5)
+            act("Tm", "T", h, None, ACT.Square, bias=-0.5)
+            act("hh", "h", h, None, ACT.Square, scale=0.5)
+            act("z2s", "z2", h, 1, ACT.Copy)
+            act("TT", "T", h, None, ACT.Square)
+
+        def tangent_products(h):
+            for i in (2, 1, 3):
+                product("tz%d" % i, "w%d" % i, "dx%d" % h)
+
+        def each_group(f):
+            for g in range(G):
+                f(g)
+
+        def gain_of(g):
+            return gain[:, g, :]
+
+        interleave("x0", True)
+        interleave("w1", False)
+        quantize("x0")
+        interleave("w2", True)
+        quantize("w1")
+        product("z1", "w1", "x0")
+        quantize("w2")
+        product("z2", "w2", "x0")
+        interleave("w3", False)
+        quantize("w3")
+        product("z3", "w3", "x0")
+        forward_copies(0)
+        each_group(lambda g: tt("m", "z1s", ALU.mult, "z2", 0, g))
+        each_group(lambda g: tt("p", "m", ALU.add, "z3", 0, g))
+        gate_functions(0)
+        interleave("dx0", True)
+        stt("Y", "h", ALU.add, 1.0, ALU.mult, "T", 0)
+        quantize("dx0")
+        tangent_products(0)
+        interleave("x1", False)
+        interleave("wo", False)
+        interleave("dy0", False)
+
+        def factors_and_tangents(h):
+            stt("nv", "Tm", ALU.add, -1.25, ALU.add, "Y", h)
+            stt("nk", "hh", ALU.add, -0.25, ALU.add, "Y", h)
+            each_group(lambda g: tt("a1", "z1s", ALU.mult, "tz2", h, g))
+            stt("F1", "hh", ALU.add, -0.25, ALU.mult, "nv", h)
+            each_group(lambda g: tt("a2", "z2s", ALU.mult, "tz1", h, g))
+            stt("F2", "TT", ALU.add, -1.0, ALU.mult, "nk", h)
+
+        factors_and_tangents(0)
+        quantize("x1")
+        forward_products(1)
+        tt("a", "a1", ALU.add, "a2", 0)
+        each_group(lambda g: tt("tF", "F2", ALU.mult, "tz3", 0, g))
+        each_group(lambda g: tt("A", "a", ALU.add, "tz3", 0, g))
+        forward_copies(1)
+        interleave("dx1", False)
+        quantize("wo")
+        quantize("dy0")
+        product("c0", "wo", "dy0")
+        each_group(lambda g: tt("m", "z1s", ALU.mult, "z2", 1, g))
+        tt("AF", "A", ALU.mult, "F1", 0)
+        each_group(lambda g: tt("p", "m", ALU.add, "z3", 1, g))
+        gate_functions(1)
+        interleave("dy1", False)
+        tt("E", "AF", ALU.add, "tF", 0)
+        quantize("dx1")
+        each_group(lambda g: stt("cE", "E", ALU.mult, gain_of(g), ALU.mult, "c0", 0, g))
+        tangent_products(1)
+        stt("Y", "h", ALU.add, 1.0, ALU.mult, "T", 1)
+        tt("res", "cE", ALU.add, "base", 0)
+        nc.sync.dma_start(out=half(out, 0).rearrange("g m c -> m g c"), in_=val("res", 0)[:])
+        factors_and_tangents(1)
+        tt("a", "a1", ALU.add, "a2", 1)
+        quantize("dy1")
+        each_group(lambda g: tt("tF", "F2", ALU.mult, "tz3", 1, g))
+        each_group(lambda g: tt("A", "a", ALU.add, "tz3", 1, g))
+        product("c0", "wo", "dy1")
+        each_group(lambda g: tt("AF", "A", ALU.mult, "F1", 1, g))
+        each_group(lambda g: tt("E", "AF", ALU.add, "tF", 1, g))
+        each_group(lambda g: stt("cE", "E", ALU.mult, gain_of(g), ALU.mult, "c0", 1, g))
+        for g in range(G):
+            tt("res", "cE", ALU.add, "base", 1, g)
+            nc.sync.dma_start(out=half(out, 1)[g], in_=val("res", 1)[:, g, :])

@@ -57,26 +57,26 @@ def tile_rows_hvbilinsig_kernel(tc, x, w1, w2, w3, wo, dy, dx, og, base, out):
             )
 
         banks = [[ps.tile([P, 2, HALF], F32, name="bank_%d_%d" % (g, b)) for b in range(4)] for g in range(G)]
-        place = {"z1": (0, 0), "tz1": (0, 1), "z2": (1, 0), "tz2": (1, 1), "z3": (2, 0), "tz3": (3, 0), "c0": (3, 1)}
+        place = {"z1": (0, 0), "z3": (0, 1), "z2": (1, 0), "tz1": (2, 0), "tz2": (2, 1), "tz3": (3, 0), "c0": (3, 1)}
 
-        def sums(name, g):
-            bank, side = place[name]
+        def sums(name, h, g):
+            bank, side = (3, 1) if (name, h) == ("z3", 0) else place[name]
             return banks[g][bank][:, side, :]
 
-        def product(name, weights, columns):
-            for g in range(G):
-                rows = slice(ROWS * g, ROWS * (g + 1))
-                for n0 in range(0, HALF, MM_N):
-                    cols = slice(n0, n0 + MM_N)
-                    nc.tensor.matmul_mx(
-                        out=sums(name, g)[:, cols],
-                        lhsT=codes[weights][rows, :].bitcast(FP8X4),
-                        lhsT_scale=scales[weights][rows, :],
-                        rhs=codes[columns][rows, cols].bitcast(FP8X4),
-                        rhs_scale=scales[columns][rows, cols],
-                        start=True,
-                        stop=True,
-                    )
+        def product(name, weights, source, h, g):
+            columns = "%s%d" % (source, h)
+            rows = slice(ROWS * g, ROWS * (g + 1))
+            for n0 in range(0, HALF, MM_N):
+                cols = slice(n0, n0 + MM_N)
+                nc.tensor.matmul_mx(
+                    out=sums(name, h, g)[:, cols],
+                    lhsT=codes[weights][rows, :].bitcast(FP8X4),
+                    lhsT_scale=scales[weights][rows, :],
+                    rhs=codes[columns][rows, cols].bitcast(FP8X4),
+                    rhs_scale=scales[columns][rows, cols],
+                    start=True,
+                    stop=True,
+                )
 
         vals = {}
 
@@ -87,14 +87,14 @@ def tile_rows_hvbilinsig_kernel(tc, x, w1, w2, w3, wo, dy, dx, og, base, out):
 
         def operand(name, h, g):
             if name in place:
-                return sums(name, g)
+                return sums(name, h, g)
             return val(name, h)[:] if g is None else val(name, h)[:, g, :]
 
         def act(dst, src, h, g, func, scale=1.0, bias=0.0):
             nc.scalar.activation(out=operand(dst, h, g), in_=operand(src, h, g), func=func, scale=scale, bias=bias)
 
-        def tt(dst, a, op, b, h, g=None):
-            nc.vector.tensor_tensor(out=operand(dst, h, g), in0=operand(a, h, g), in1=operand(b, h, g), op=op)
+        def tt(dst, a, op, b, h, g=None, engine=nc.vector):
+            engine.tensor_tensor(out=operand(dst, h, g), in0=operand(a, h, g), in1=operand(b, h, g), op=op)
 
         def stt(dst, a, op0, scalar, op1, b, h, g=None):
             nc.vector.scalar_tensor_tensor(
@@ -109,41 +109,20 @@ def tile_rows_hvbilinsig_kernel(tc, x, w1, w2, w3, wo, dy, dx, og, base, out):
 
         load("x0", half(x, 0))
         load("w1", w1)
-        load("w2", w2)
         load("w3", w3)
+        load("w2", w2)
         load("dx0", half(dx, 0))
-        load("x1", half(x, 1))
         load("wo", wo)
+        load("x1", half(x, 1))
+        load("dx1", half(dx, 1))
         load("dy0", half(dy, 0))
         gain = sb.tile([P, G, 1], F32, name="gain")
         with nc.allow_non_contiguous_dma(reason="one gain a partition and group"):
             nc.sync.dma_start(out=gain[:], in_=og.rearrange("g m o -> m g o"))
-        load("dx1", half(dx, 1))
         load_base(0)
         load("dy1", half(dy, 1))
         load_base(1)
-
-        def forward_products(h):
-            for i in (1, 2, 3):
-                product("z%d" % i, "w%d" % i, "x%d" % h)
-
-        def forward_copies(h):
-            for g in range(G):
-                act("z1s", "z1", h, g, ACT.Copy)
-            for g in range(G):
-                act("T", "z3", h, g, ACT.Tanh)
-
-        def gate_functions(h):
-            act("z2s", "z2", h, 0, ACT.Copy)
-            act("h", "p", h, None, ACT.Tanh, scale=0.5)
-            act("Tm", "T", h, None, ACT.Square, bias=-0.5)
-            act("hh", "h", h, None, ACT.Square, scale=0.5)
-            act("z2s", "z2", h, 1, ACT.Copy)
-            act("TT", "T", h, None, ACT.Square)
-
-        def tangent_products(h):
-            for i in (2, 1, 3):
-                product("tz%d" % i, "w%d" % i, "dx%d" % h)
+        side = nc.gpsimd
 
         def each_group(f):
             for g in range(G):
@@ -152,66 +131,96 @@ def tile_rows_hvbilinsig_kernel(tc, x, w1, w2, w3, wo, dy, dx, og, base, out):
         def gain_of(g):
             return gain[:, g, :]
 
+        def tangent_terms(h, g):
+            tt("a1", "z1s", ALU.mult, "tz2", h, g)
+            tt("a2", "z2s", ALU.mult, "tz1", h, g)
+            tt("a3", "a1", ALU.add, "tz3", h, g)
+
         interleave("x0", True)
         interleave("w1", False)
         quantize("x0")
-        interleave("w2", True)
+        interleave("w3", True)
         quantize("w1")
-        product("z1", "w1", "x0")
-        quantize("w2")
-        product("z2", "w2", "x0")
-        interleave("w3", False)
+        each_group(lambda g: product("z1", "w1", "x", 0, g))
+        interleave("w2", True)
         quantize("w3")
-        product("z3", "w3", "x0")
-        forward_copies(0)
-        each_group(lambda g: tt("m", "z1s", ALU.mult, "z2", 0, g))
-        each_group(lambda g: tt("p", "m", ALU.add, "z3", 0, g))
-        gate_functions(0)
+        quantize("w2")
+        product("z3", "w3", "x", 0, 0)
+        each_group(lambda g: product("z2", "w2", "x", 0, g))
+        product("z3", "w3", "x", 0, 1)
+        each_group(lambda g: act("z1s", "z1", 0, g, ACT.Copy))
+        each_group(lambda g: act("T", "z3", 0, g, ACT.Tanh))
         interleave("dx0", True)
-        stt("Y", "h", ALU.add, 1.0, ALU.mult, "T", 0)
+        each_group(lambda g: tt("m", "z1s", ALU.mult, "z2", 0, g))
         quantize("dx0")
-        tangent_products(0)
+        each_group(lambda g: tt("p", "m", ALU.add, "z3", 0, g))
+        for g in range(G):
+            product("tz2", "w2", "dx", 0, g)
+            product("tz1", "w1", "dx", 0, g)
+            product("tz3", "w3", "dx", 0, g)
+        each_group(lambda g: act("z2s", "z2", 0, g, ACT.Copy))
+        each_group(lambda g: act("h", "p", 0, g, ACT.Tanh, scale=0.5))
+        act("Tm", "T", 0, None, ACT.Square, bias=-0.5)
+        act("hh", "h", 0, None, ACT.Square, scale=0.5)
         interleave("x1", False)
-        interleave("wo", False)
-        interleave("dy0", False)
-
-        def factors_and_tangents(h):
-            stt("nv", "Tm", ALU.add, -1.25, ALU.add, "Y", h)
-            stt("nk", "hh", ALU.add, -0.25, ALU.add, "Y", h)
-            each_group(lambda g: tt("a1", "z1s", ALU.mult, "tz2", h, g))
-            stt("F1", "hh", ALU.add, -0.25, ALU.mult, "nv", h)
-            each_group(lambda g: tt("a2", "z2s", ALU.mult, "tz1", h, g))
-            stt("F2", "TT", ALU.add, -1.0, ALU.mult, "nk", h)
-
-        factors_and_tangents(0)
-        quantize("x1")
-        forward_products(1)
-        tt("a", "a1", ALU.add, "a2", 0)
-        each_group(lambda g: tt("tF", "F2", ALU.mult, "tz3", 0, g))
-        each_group(lambda g: tt("A", "a", ALU.add, "tz3", 0, g))
-        forward_copies(1)
+        act("TT", "T", 0, None, ACT.Square)
         interleave("dx1", False)
+        interleave("dy0", False)
+        interleave("wo", True)
+        tt("a1", "z1s", ALU.mult, "tz2", 0, 0)
         quantize("wo")
-        quantize("dy0")
-        product("c0", "wo", "dy0")
-        each_group(lambda g: tt("m", "z1s", ALU.mult, "z2", 1, g))
-        tt("AF", "A", ALU.mult, "F1", 0)
-        each_group(lambda g: tt("p", "m", ALU.add, "z3", 1, g))
-        gate_functions(1)
-        interleave("dy1", False)
-        tt("E", "AF", ALU.add, "tF", 0)
+        tt("a2", "z2s", ALU.mult, "tz1", 0, 0)
+        stt("Y", "h", ALU.add, 1.0, ALU.mult, "T", 0)
+        tt("a3", "a1", ALU.add, "tz3", 0, 0)
+        tt("A", "a3", ALU.add, "a2", 0, 0, side)
+        tangent_terms(0, 1)
+        stt("nv", "Tm", ALU.add, -1.25, ALU.add, "Y", 0)
+        quantize("x1")
+        for g in range(G):
+            product("z1", "w1", "x", 1, g)
+            product("z3", "w3", "x", 1, g)
+        each_group(lambda g: product("z2", "w2", "x", 1, g))
+        stt("nk", "hh", ALU.add, -0.25, ALU.add, "Y", 0)
+        tt("A", "a3", ALU.add, "a2", 0, 1)
+        stt("F2", "TT", ALU.add, -1.0, ALU.mult, "nk", 0)
         quantize("dx1")
+        stt("F1", "hh", ALU.add, -0.25, ALU.mult, "nv", 0)
+        quantize("dy0")
+        for g in range(G):
+            product("tz2", "w2", "dx", 1, g)
+            product("tz1", "w1", "dx", 1, g)
+        for g in range(G):
+            act("z1s", "z1", 1, g, ACT.Copy)
+            act("T", "z3", 1, g, ACT.Tanh)
+        each_group(lambda g: tt("AF", "A", ALU.mult, "F1", 0, g, side))
+        each_group(lambda g: tt("tF", "F2", ALU.mult, "tz3", 0, g))
+        for g in range(G):
+            product("tz3", "w3", "dx", 1, g)
+            product("c0", "wo", "dy", 0, g)
+        each_group(lambda g: tt("E", "AF", ALU.add, "tF", 0, g, side))
+        each_group(lambda g: tt("m", "z1s", ALU.mult, "z2", 1, g))
+        each_group(lambda g: tt("p", "m", ALU.add, "z3", 1, g))
+        each_group(lambda g: act("z2s", "z2", 1, g, ACT.Copy))
+        act("h", "p", 1, None, ACT.Tanh, scale=0.5)
+        act("Tm", "T", 1, None, ACT.Square, bias=-0.5)
+        act("hh", "h", 1, None, ACT.Square, scale=0.5)
+        act("TT", "T", 1, None, ACT.Square)
+        interleave("dy1", False)
+        tangent_terms(1, 0)
+        tt("A", "a3", ALU.add, "a2", 1, 0, side)
+        tangent_terms(1, 1)
         each_group(lambda g: stt("cE", "E", ALU.mult, gain_of(g), ALU.mult, "c0", 0, g))
-        tangent_products(1)
         stt("Y", "h", ALU.add, 1.0, ALU.mult, "T", 1)
+        tt("A", "a3", ALU.add, "a2", 1, 1)
+        stt("nv", "Tm", ALU.add, -1.25, ALU.add, "Y", 1)
+        stt("nk", "hh", ALU.add, -0.25, ALU.add, "Y", 1)
         tt("res", "cE", ALU.add, "base", 0)
         nc.sync.dma_start(out=half(out, 0).rearrange("g m c -> m g c"), in_=val("res", 0)[:])
-        factors_and_tangents(1)
-        tt("a", "a1", ALU.add, "a2", 1)
+        stt("F2", "TT", ALU.add, -1.0, ALU.mult, "nk", 1)
+        stt("F1", "hh", ALU.add, -0.25, ALU.mult, "nv", 1)
         quantize("dy1")
         each_group(lambda g: tt("tF", "F2", ALU.mult, "tz3", 1, g))
-        each_group(lambda g: tt("A", "a", ALU.add, "tz3", 1, g))
-        product("c0", "wo", "dy1")
+        each_group(lambda g: product("c0", "wo", "dy", 1, g))
         each_group(lambda g: tt("AF", "A", ALU.mult, "F1", 1, g))
         each_group(lambda g: tt("E", "AF", ALU.add, "tF", 1, g))
         each_group(lambda g: stt("cE", "E", ALU.mult, gain_of(g), ALU.mult, "c0", 1, g))

@@ -34,14 +34,24 @@ def tile_rows_hvbilinsig_kernel(tc, x, w1, w2, w3, wo, dy, dx, og, base, out):
         def load(key, src):
             width = src.shape[2]
             raw[key] = sb.tile([P, PACK, width], F32, name="raw_" + key)
+            packed[key] = sb.tile([P, width * PACK], BF16, name="packed_" + key, align_bytes=64)
             nc.sync.dma_start(out=raw[key][:], in_=src.rearrange("g (p j) c -> (g p) j c", j=PACK))
 
-        def interleave(key, on_vector):
-            width = raw[key].shape[2]
-            packed[key] = sb.tile([P, width, PACK], BF16, name="packed_" + key, align_bytes=64)
-            dst = packed[key][:].rearrange("p (c i) j -> p c j i", i=LINE)
-            src = raw[key][:].rearrange("p j (c i) -> p c j i", i=LINE)
-            if on_vector:
+        def interleave(key, engine, c0=0, c1=None):
+            c1 = raw[key].shape[2] if c1 is None else c1
+            if engine == "gpsimd":
+                nc.gpsimd.tensor_scalar(
+                    out=packed[key][:, PACK * c0 : PACK * c1].rearrange("p (c j) -> p c j", j=PACK),
+                    in0=raw[key][:, :, c0:c1].rearrange("p j c -> p c j"),
+                    scalar1=1.0,
+                    scalar2=0.0,
+                    op0=ALU.mult,
+                    op1=ALU.add,
+                )
+                return
+            dst = packed[key][:, PACK * c0 : PACK * c1].rearrange("p (c i j) -> p c j i", i=LINE, j=PACK)
+            src = raw[key][:, :, c0:c1].rearrange("p j (c i) -> p c j i", i=LINE)
+            if engine == "vector":
                 nc.vector.tensor_copy(out=dst, in_=src)
             else:
                 nc.scalar.activation(out=dst, in_=src, func=ACT.Copy)
@@ -50,45 +60,60 @@ def tile_rows_hvbilinsig_kernel(tc, x, w1, w2, w3, wo, dy, dx, og, base, out):
             width = raw[key].shape[2]
             codes[key] = sb.tile([P, width], U32, name="codes_" + key, align_bytes=64)
             scales[key] = sb.tile([P, width], U8, name="scales_" + key, align_bytes=64)
-            nc.vector.quantize_mx(
-                out=codes[key][:].bitcast(FP8X4),
-                scales=scales[key][:],
-                in_=packed[key][:].rearrange("p c j -> p (c j)"),
-            )
+            nc.vector.quantize_mx(out=codes[key][:].bitcast(FP8X4), scales=scales[key][:], in_=packed[key][:])
 
         banks = [[ps.tile([P, 2, HALF], F32, name="bank_%d_%d" % (g, b)) for b in range(4)] for g in range(G)]
-        place = {"z1": (0, 0), "z3": (0, 1), "z2": (1, 0), "tz1": (2, 0), "tz2": (2, 1), "tz3": (3, 0), "c0": (3, 1)}
+        place = {"z1": (0, 0), "z3": (0, 1), "z2": (1, 0), "tz2": (2, 0), "tz1": (2, 1), "tz3": (3, 0), "c0": (1, 1)}
 
         def sums(name, h, g):
             bank, side = (3, 1) if (name, h) == ("z3", 0) else place[name]
             return banks[g][bank][:, side, :]
 
-        def product(name, weights, source, h, g):
+        def product(name, weights, source, h):
             columns = "%s%d" % (source, h)
-            rows = slice(ROWS * g, ROWS * (g + 1))
             for n0 in range(0, HALF, MM_N):
                 cols = slice(n0, n0 + MM_N)
-                nc.tensor.matmul_mx(
-                    out=sums(name, h, g)[:, cols],
-                    lhsT=codes[weights][rows, :].bitcast(FP8X4),
-                    lhsT_scale=scales[weights][rows, :],
-                    rhs=codes[columns][rows, cols].bitcast(FP8X4),
-                    rhs_scale=scales[columns][rows, cols],
-                    start=True,
-                    stop=True,
-                )
+                for g in range(G):
+                    rows = slice(ROWS * g, ROWS * (g + 1))
+                    nc.tensor.matmul_mx(
+                        out=sums(name, h, g)[:, cols],
+                        lhsT=codes[weights][rows, :].bitcast(FP8X4),
+                        lhsT_scale=scales[weights][rows, :],
+                        rhs=codes[columns][rows, cols].bitcast(FP8X4),
+                        rhs_scale=scales[columns][rows, cols],
+                        start=True,
+                        stop=True,
+                    )
 
+        by_group = {"z1s": ("zs", 0), "z2s": ("zs", 1), "a1": ("a12", 0), "a2": ("a12", 1)}
+        by_value = {"h": ("hT", 0), "T": ("hT", 1), "hh": ("sq", 0), "TT": ("sq", 1),
+                    "nv": ("nvk", 0), "nk": ("nvk", 1), "F1": ("F12", 0), "F2": ("F12", 1)}
         vals = {}
 
-        def val(name, h):
+        def val(name, h, shape):
             if (name, h) not in vals:
-                vals[(name, h)] = sb.tile([P, G, HALF], F32, name="%s_%d" % (name, h))
+                vals[(name, h)] = sb.tile(shape, F32, name="%s_%d" % (name, h))
             return vals[(name, h)]
 
         def operand(name, h, g):
             if name in place:
                 return sums(name, h, g)
-            return val(name, h)[:] if g is None else val(name, h)[:, g, :]
+            if name == "tz21":
+                return banks[g][2][:].rearrange("p s c -> p (s c)")
+            if name in ("zs", "a12"):
+                return val(name, h, [P, G, 2, HALF])[:, g, :, :].rearrange("p s c -> p (s c)")
+            if name in by_group:
+                pair, slot = by_group[name]
+                t = val(pair, h, [P, G, 2, HALF])
+                return t[:, :, slot, :] if g is None else t[:, g, slot, :]
+            if name in ("hT", "sq", "nvk", "F12"):
+                return val(name, h, [P, 2, G, HALF])[:].rearrange("p s g c -> p (s g c)")
+            if name in by_value:
+                pair, slot = by_value[name]
+                t = val(pair, h, [P, 2, G, HALF])
+                return t[:, slot, :, :] if g is None else t[:, slot, g, :]
+            t = val(name, h, [P, G, HALF])
+            return t[:] if g is None else t[:, g, :]
 
         def act(dst, src, h, g, func, scale=1.0, bias=0.0):
             nc.scalar.activation(out=operand(dst, h, g), in_=operand(src, h, g), func=func, scale=scale, bias=bias)
@@ -105,7 +130,7 @@ def tile_rows_hvbilinsig_kernel(tc, x, w1, w2, w3, wo, dy, dx, og, base, out):
             return t[:, :, h * HALF : (h + 1) * HALF]
 
         def load_base(h):
-            nc.sync.dma_start(out=val("base", h)[:], in_=half(base, h).rearrange("g m c -> m g c"))
+            nc.sync.dma_start(out=operand("base", h, None), in_=half(base, h).rearrange("g m c -> m g c"))
 
         load("x0", half(x, 0))
         load("w1", w1)
@@ -131,99 +156,88 @@ def tile_rows_hvbilinsig_kernel(tc, x, w1, w2, w3, wo, dy, dx, og, base, out):
         def gain_of(g):
             return gain[:, g, :]
 
-        def tangent_terms(h, g):
-            tt("a1", "z1s", ALU.mult, "tz2", h, g)
-            tt("a2", "z2s", ALU.mult, "tz1", h, g)
-            tt("a3", "a1", ALU.add, "tz3", h, g)
-
-        interleave("x0", True)
-        interleave("w1", False)
+        interleave("x0", "vector")
+        interleave("w1", "vector")
+        interleave("w3", "scalar")
         quantize("x0")
-        interleave("w3", True)
         quantize("w1")
-        each_group(lambda g: product("z1", "w1", "x", 0, g))
-        interleave("w2", True)
+        product("z1", "w1", "x", 0)
+        interleave("w2", "vector")
         quantize("w3")
         quantize("w2")
-        product("z3", "w3", "x", 0, 0)
-        each_group(lambda g: product("z2", "w2", "x", 0, g))
-        product("z3", "w3", "x", 0, 1)
+        product("z3", "w3", "x", 0)
+        product("z2", "w2", "x", 0)
         each_group(lambda g: act("z1s", "z1", 0, g, ACT.Copy))
         each_group(lambda g: act("T", "z3", 0, g, ACT.Tanh))
-        interleave("dx0", True)
-        each_group(lambda g: tt("m", "z1s", ALU.mult, "z2", 0, g))
-        quantize("dx0")
-        each_group(lambda g: tt("p", "m", ALU.add, "z3", 0, g))
-        for g in range(G):
-            product("tz2", "w2", "dx", 0, g)
-            product("tz1", "w1", "dx", 0, g)
-            product("tz3", "w3", "dx", 0, g)
-        each_group(lambda g: act("z2s", "z2", 0, g, ACT.Copy))
-        each_group(lambda g: act("h", "p", 0, g, ACT.Tanh, scale=0.5))
         act("Tm", "T", 0, None, ACT.Square, bias=-0.5)
+        interleave("dx0", "vector")
+        quantize("dx0")
+        each_group(lambda g: tt("m", "z1s", ALU.mult, "z2", 0, g))
+        each_group(lambda g: tt("p", "m", ALU.add, "z3", 0, g))
+        product("tz2", "w2", "dx", 0)
+        product("tz1", "w1", "dx", 0)
+        product("tz3", "w3", "dx", 0)
+        each_group(lambda g: act("z2s", "z2", 0, g, ACT.Copy))
+        interleave("x1", "scalar")
+        act("h", "p", 0, None, ACT.Tanh, scale=0.5)
+        act("TT", "T", 0, None, ACT.Square, scale=0.5)
         act("hh", "h", 0, None, ACT.Square, scale=0.5)
-        interleave("x1", False)
-        act("TT", "T", 0, None, ACT.Square)
-        interleave("dx1", False)
-        interleave("dy0", False)
-        interleave("wo", True)
-        tt("a1", "z1s", ALU.mult, "tz2", 0, 0)
+        interleave("dx1", "scalar")
+        interleave("dy0", "scalar")
+        interleave("wo", "vector")
+        tt("a12", "zs", ALU.mult, "tz21", 0, 0)
         quantize("wo")
-        tt("a2", "z2s", ALU.mult, "tz1", 0, 0)
-        stt("Y", "h", ALU.add, 1.0, ALU.mult, "T", 0)
         tt("a3", "a1", ALU.add, "tz3", 0, 0)
         tt("A", "a3", ALU.add, "a2", 0, 0, side)
-        tangent_terms(0, 1)
-        stt("nv", "Tm", ALU.add, -1.25, ALU.add, "Y", 0)
+        tt("a1", "z1s", ALU.mult, "tz2", 0, 1)
+        tt("a2", "z2s", ALU.mult, "tz1", 0, 1)
+        tt("a3", "a1", ALU.add, "tz3", 0, 1)
+        stt("Y", "h", ALU.add, 1.0, ALU.mult, "T", 0)
         quantize("x1")
-        for g in range(G):
-            product("z1", "w1", "x", 1, g)
-            product("z3", "w3", "x", 1, g)
-        each_group(lambda g: product("z2", "w2", "x", 1, g))
+        product("z1", "w1", "x", 1)
+        product("z3", "w3", "x", 1)
+        product("z2", "w2", "x", 1)
+        stt("nv", "Tm", ALU.add, -1.25, ALU.add, "Y", 0)
         stt("nk", "hh", ALU.add, -0.25, ALU.add, "Y", 0)
         tt("A", "a3", ALU.add, "a2", 0, 1)
-        stt("F2", "TT", ALU.add, -1.0, ALU.mult, "nk", 0)
         quantize("dx1")
-        stt("F1", "hh", ALU.add, -0.25, ALU.mult, "nv", 0)
+        product("tz2", "w2", "dx", 1)
+        product("tz1", "w1", "dx", 1)
+        stt("F12", "sq", ALU.add, -0.25, ALU.mult, "nvk", 0)
         quantize("dy0")
-        for g in range(G):
-            product("tz2", "w2", "dx", 1, g)
-            product("tz1", "w1", "dx", 1, g)
         for g in range(G):
             act("z1s", "z1", 1, g, ACT.Copy)
             act("T", "z3", 1, g, ACT.Tanh)
-        each_group(lambda g: tt("AF", "A", ALU.mult, "F1", 0, g, side))
-        each_group(lambda g: tt("tF", "F2", ALU.mult, "tz3", 0, g))
-        for g in range(G):
-            product("tz3", "w3", "dx", 1, g)
-            product("c0", "wo", "dy", 0, g)
-        each_group(lambda g: tt("E", "AF", ALU.add, "tF", 0, g, side))
+        each_group(lambda g: stt("tF", "F2", ALU.mult, 4.0, ALU.mult, "tz3", 0, g))
+        tt("AF", "A", ALU.mult, "F1", 0, None, side)
+        tt("E", "AF", ALU.add, "tF", 0, None, side)
+        product("tz3", "w3", "dx", 1)
         each_group(lambda g: tt("m", "z1s", ALU.mult, "z2", 1, g))
         each_group(lambda g: tt("p", "m", ALU.add, "z3", 1, g))
         each_group(lambda g: act("z2s", "z2", 1, g, ACT.Copy))
+        product("c0", "wo", "dy", 0)
         act("h", "p", 1, None, ACT.Tanh, scale=0.5)
         act("Tm", "T", 1, None, ACT.Square, bias=-0.5)
-        act("hh", "h", 1, None, ACT.Square, scale=0.5)
-        act("TT", "T", 1, None, ACT.Square)
-        interleave("dy1", False)
-        tangent_terms(1, 0)
+        act("sq", "hT", 1, None, ACT.Square, scale=0.5)
+        interleave("dy1", "scalar")
+        each_group(lambda g: tt("a12", "zs", ALU.mult, "tz21", 1, g))
+        tt("a3", "a1", ALU.add, "tz3", 1, 0)
         tt("A", "a3", ALU.add, "a2", 1, 0, side)
-        tangent_terms(1, 1)
+        tt("a3", "a1", ALU.add, "tz3", 1, 1)
         each_group(lambda g: stt("cE", "E", ALU.mult, gain_of(g), ALU.mult, "c0", 0, g))
         stt("Y", "h", ALU.add, 1.0, ALU.mult, "T", 1)
         tt("A", "a3", ALU.add, "a2", 1, 1)
         stt("nv", "Tm", ALU.add, -1.25, ALU.add, "Y", 1)
         stt("nk", "hh", ALU.add, -0.25, ALU.add, "Y", 1)
         tt("res", "cE", ALU.add, "base", 0)
-        nc.sync.dma_start(out=half(out, 0).rearrange("g m c -> m g c"), in_=val("res", 0)[:])
-        stt("F2", "TT", ALU.add, -1.0, ALU.mult, "nk", 1)
-        stt("F1", "hh", ALU.add, -0.25, ALU.mult, "nv", 1)
+        nc.sync.dma_start(out=half(out, 0).rearrange("g m c -> m g c"), in_=operand("res", 0, None))
+        stt("F12", "sq", ALU.add, -0.25, ALU.mult, "nvk", 1)
         quantize("dy1")
-        each_group(lambda g: tt("tF", "F2", ALU.mult, "tz3", 1, g))
-        each_group(lambda g: product("c0", "wo", "dy", 1, g))
-        each_group(lambda g: tt("AF", "A", ALU.mult, "F1", 1, g))
+        product("c0", "wo", "dy", 1)
+        tt("AF", "A", ALU.mult, "F1", 1)
+        each_group(lambda g: stt("tF", "F2", ALU.mult, 4.0, ALU.mult, "tz3", 1, g))
         each_group(lambda g: tt("E", "AF", ALU.add, "tF", 1, g))
         each_group(lambda g: stt("cE", "E", ALU.mult, gain_of(g), ALU.mult, "c0", 1, g))
         for g in range(G):
             tt("res", "cE", ALU.add, "base", 1, g)
-            nc.sync.dma_start(out=half(out, 1)[g], in_=val("res", 1)[:, g, :])
+            nc.sync.dma_start(out=half(out, 1)[g], in_=operand("res", 1, g))

@@ -11,14 +11,21 @@ U32 = mybir.dt.uint32
 U8 = mybir.dt.uint8
 FP8X4 = mybir.dt.float8_e4m3fn_x4
 ACT = mybir.ActivationFunctionType
-ALU = mybir.AluOpType
+ADD = mybir.AluOpType.add
+MULT = mybir.AluOpType.mult
 
 P = 128
 PACK = 4
 ROWS = D // PACK
 HALF = N // 2
 MM_N = 128
-LINE = 4
+RUN = 4
+
+PLACE = {"z1": (0, 0), "z3": (0, 1), "z2": (1, 0), "c0": (1, 1), "tz2": (2, 0), "tz1": (2, 1), "tz3": (3, 0)}
+MOVED = {("z3", 0): (3, 1), ("c0", 1): (2, 0)}
+
+GROUP_PAIRS = {"z1z2": ("z1_sb", "z2_sb"), "cross": ("z1_tz2", "z2_tz1")}
+WIDE_PAIRS = {"HT": ("H", "T"), "squares": ("H_sq", "T_sq"), "VK": ("V", "K"), "F": ("F1", "F2")}
 
 
 def tile_rows_hvbilinsig_kernel(tc, x, w1, w2, w3, wo, dy, dx, og, base, out):
@@ -29,215 +36,216 @@ def tile_rows_hvbilinsig_kernel(tc, x, w1, w2, w3, wo, dy, dx, og, base, out):
         ps = ctx.enter_context(tc.psum_pool(name="ps", bufs=1))
         ctx.enter_context(tc.manual_schedule())
 
-        raw, packed, codes, scales = {}, {}, {}, {}
+        raw, rounded, codes, scales = {}, {}, {}, {}
 
-        def load(key, src):
+        def columns(tensor, half):
+            return tensor[:, :, half * HALF : (half + 1) * HALF]
+
+        def load(name, src):
             width = src.shape[2]
-            raw[key] = sb.tile([P, PACK, width], F32, name="raw_" + key)
-            packed[key] = sb.tile([P, width * PACK], BF16, name="packed_" + key, align_bytes=64)
-            nc.sync.dma_start(out=raw[key][:], in_=src.rearrange("g (p j) c -> (g p) j c", j=PACK))
+            raw[name] = sb.tile([P, PACK, width], F32, name="raw_" + name)
+            rounded[name] = sb.tile([P, width * PACK], BF16, name="rounded_" + name, align_bytes=64)
+            nc.sync.dma_start(out=raw[name][:], in_=src.rearrange("g (p j) c -> (g p) j c", j=PACK))
 
-        def interleave(key, engine, c0=0, c1=None):
-            c1 = raw[key].shape[2] if c1 is None else c1
-            if engine == "gpsimd":
-                nc.gpsimd.tensor_scalar(
-                    out=packed[key][:, PACK * c0 : PACK * c1].rearrange("p (c j) -> p c j", j=PACK),
-                    in0=raw[key][:, :, c0:c1].rearrange("p j c -> p c j"),
-                    scalar1=1.0,
-                    scalar2=0.0,
-                    op0=ALU.mult,
-                    op1=ALU.add,
-                )
-                return
-            dst = packed[key][:, PACK * c0 : PACK * c1].rearrange("p (c i j) -> p c j i", i=LINE, j=PACK)
-            src = raw[key][:, :, c0:c1].rearrange("p j (c i) -> p c j i", i=LINE)
-            if engine == "vector":
-                nc.vector.tensor_copy(out=dst, in_=src)
-            else:
-                nc.scalar.activation(out=dst, in_=src, func=ACT.Copy)
+        def rounding_views(name, c0, c1):
+            dst = rounded[name][:, PACK * c0 : PACK * c1].rearrange("p (c i j) -> p c j i", i=RUN, j=PACK)
+            src = raw[name][:, :, c0:c1].rearrange("p j (c i) -> p c j i", i=RUN)
+            return dst, src
 
-        def quantize(key):
-            width = raw[key].shape[2]
-            codes[key] = sb.tile([P, width], U32, name="codes_" + key, align_bytes=64)
-            scales[key] = sb.tile([P, width], U8, name="scales_" + key, align_bytes=64)
-            nc.vector.quantize_mx(out=codes[key][:].bitcast(FP8X4), scales=scales[key][:], in_=packed[key][:])
+        def round_on_vector(name):
+            dst, src = rounding_views(name, 0, raw[name].shape[2])
+            nc.vector.tensor_copy(out=dst, in_=src)
+
+        def round_on_scalar(name, c0, c1):
+            dst, src = rounding_views(name, c0, c1)
+            nc.scalar.activation(out=dst, in_=src, func=ACT.Copy)
+
+        def quantize(name):
+            width = raw[name].shape[2]
+            codes[name] = sb.tile([P, width], U32, name="codes_" + name, align_bytes=64)
+            scales[name] = sb.tile([P, width], U8, name="scales_" + name, align_bytes=64)
+            nc.vector.quantize_mx(out=codes[name][:].bitcast(FP8X4), scales=scales[name][:], in_=rounded[name][:])
 
         banks = [[ps.tile([P, 2, HALF], F32, name="bank_%d_%d" % (g, b)) for b in range(4)] for g in range(G)]
-        place = {"z1": (0, 0), "z3": (0, 1), "z2": (1, 0), "tz2": (2, 0), "tz1": (2, 1), "tz3": (3, 0), "c0": (1, 1)}
 
-        def sums(name, h, g):
-            bank, side = (3, 1) if (name, h) == ("z3", 0) else place[name]
+        def sums(name, half, g):
+            bank, side = MOVED.get((name, half), PLACE[name])
             return banks[g][bank][:, side, :]
 
-        def product(name, weights, source, h):
-            columns = "%s%d" % (source, h)
+        def product(name, weights, source, half):
+            moving = "%s%d" % (source, half)
             for n0 in range(0, HALF, MM_N):
                 cols = slice(n0, n0 + MM_N)
                 for g in range(G):
                     rows = slice(ROWS * g, ROWS * (g + 1))
                     nc.tensor.matmul_mx(
-                        out=sums(name, h, g)[:, cols],
+                        out=sums(name, half, g)[:, cols],
                         lhsT=codes[weights][rows, :].bitcast(FP8X4),
                         lhsT_scale=scales[weights][rows, :],
-                        rhs=codes[columns][rows, cols].bitcast(FP8X4),
-                        rhs_scale=scales[columns][rows, cols],
+                        rhs=codes[moving][rows, cols].bitcast(FP8X4),
+                        rhs_scale=scales[moving][rows, cols],
                         start=True,
                         stop=True,
                     )
 
-        by_group = {"z1s": ("zs", 0), "z2s": ("zs", 1), "a1": ("a12", 0), "a2": ("a12", 1)}
-        by_value = {"h": ("hT", 0), "T": ("hT", 1), "hh": ("sq", 0), "TT": ("sq", 1),
-                    "nv": ("nvk", 0), "nk": ("nvk", 1), "F1": ("F12", 0), "F2": ("F12", 1)}
-        vals = {}
+        tiles = {}
 
-        def val(name, h, shape):
-            if (name, h) not in vals:
-                vals[(name, h)] = sb.tile(shape, F32, name="%s_%d" % (name, h))
-            return vals[(name, h)]
+        def tile_of(name, half, shape):
+            if (name, half) not in tiles:
+                tiles[(name, half)] = sb.tile(shape, F32, name="%s_%d" % (name, half))
+            return tiles[(name, half)]
 
-        def operand(name, h, g):
-            if name in place:
-                return sums(name, h, g)
-            if name == "tz21":
-                return banks[g][2][:].rearrange("p s c -> p (s c)")
-            if name in ("zs", "a12"):
-                return val(name, h, [P, G, 2, HALF])[:, g, :, :].rearrange("p s c -> p (s c)")
-            if name in by_group:
-                pair, slot = by_group[name]
-                t = val(pair, h, [P, G, 2, HALF])
-                return t[:, :, slot, :] if g is None else t[:, g, slot, :]
-            if name in ("hT", "sq", "nvk", "F12"):
-                return val(name, h, [P, 2, G, HALF])[:].rearrange("p s g c -> p (s g c)")
-            if name in by_value:
-                pair, slot = by_value[name]
-                t = val(pair, h, [P, 2, G, HALF])
-                return t[:, slot, :, :] if g is None else t[:, slot, g, :]
-            t = val(name, h, [P, G, HALF])
-            return t[:] if g is None else t[:, g, :]
+        def value(name, half, g):
+            group = slice(None) if g is None else g
+            if name in PLACE:
+                return sums(name, half, g)
+            if name == "tz2tz1":
+                return banks[g][PLACE["tz2"][0]][:].rearrange("p s c -> p (s c)")
+            if name in GROUP_PAIRS:
+                return tile_of(name, half, [P, G, 2, HALF])[:, g, :, :].rearrange("p s c -> p (s c)")
+            if name in WIDE_PAIRS:
+                return tile_of(name, half, [P, 2, G, HALF])[:].rearrange("p s g c -> p (s g c)")
+            for pair, members in GROUP_PAIRS.items():
+                if name in members:
+                    return tile_of(pair, half, [P, G, 2, HALF])[:, group, members.index(name), :]
+            for pair, members in WIDE_PAIRS.items():
+                if name in members:
+                    return tile_of(pair, half, [P, 2, G, HALF])[:, members.index(name), group, :]
+            return tile_of(name, half, [P, G, HALF])[:, group, :]
 
-        def act(dst, src, h, g, func, scale=1.0, bias=0.0):
-            nc.scalar.activation(out=operand(dst, h, g), in_=operand(src, h, g), func=func, scale=scale, bias=bias)
+        def unary(dst, func, src, half, g=None, scale=1.0, bias=0.0):
+            nc.scalar.activation(out=value(dst, half, g), in_=value(src, half, g), func=func, scale=scale, bias=bias)
 
-        def tt(dst, a, op, b, h, g=None, engine=nc.vector):
-            engine.tensor_tensor(out=operand(dst, h, g), in0=operand(a, h, g), in1=operand(b, h, g), op=op)
+        def binary(dst, a, op, b, half, g=None, engine=nc.vector):
+            engine.tensor_tensor(out=value(dst, half, g), in0=value(a, half, g), in1=value(b, half, g), op=op)
 
-        def stt(dst, a, op0, scalar, op1, b, h, g=None):
+        def fused(dst, a, op0, scalar, op1, b, half, g=None):
             nc.vector.scalar_tensor_tensor(
-                out=operand(dst, h, g), in0=operand(a, h, g), scalar=scalar, in1=operand(b, h, g), op0=op0, op1=op1
+                out=value(dst, half, g),
+                in0=value(a, half, g),
+                scalar=scalar,
+                in1=value(b, half, g),
+                op0=op0,
+                op1=op1,
             )
 
-        def half(t, h):
-            return t[:, :, h * HALF : (h + 1) * HALF]
+        def unary_each(dst, func, src, half):
+            for g in range(G):
+                unary(dst, func, src, half, g)
 
-        def load_base(h):
-            nc.sync.dma_start(out=operand("base", h, None), in_=half(base, h).rearrange("g m c -> m g c"))
+        def binary_each(dst, a, op, b, half):
+            for g in range(G):
+                binary(dst, a, op, b, half, g)
 
-        load("x0", half(x, 0))
+        def tz3_term(half):
+            for g in range(G):
+                fused("tz3_F2", "F2", MULT, 4.0, MULT, "tz3", half, g)
+
+        def upstream_term(half):
+            for g in range(G):
+                fused("og_c0_E", "E", MULT, gain[:, g, :], MULT, "c0", half, g)
+
+        def factors(half):
+            fused("V", "T_shift_sq", ADD, -1.25, ADD, "Y", half)
+            fused("K", "H_sq", ADD, -0.25, ADD, "Y", half)
+            binary("A", "z1_tz2_tz3", ADD, "z2_tz1", half)
+
+        load("x0", columns(x, 0))
         load("w1", w1)
         load("w3", w3)
         load("w2", w2)
-        load("dx0", half(dx, 0))
+        load("dx0", columns(dx, 0))
         load("wo", wo)
-        load("x1", half(x, 1))
-        load("dx1", half(dx, 1))
-        load("dy0", half(dy, 0))
+        load("x1", columns(x, 1))
+        load("dx1", columns(dx, 1))
+        load("dy0", columns(dy, 0))
         gain = sb.tile([P, G, 1], F32, name="gain")
-        with nc.allow_non_contiguous_dma(reason="one gain a partition and group"):
+        with nc.allow_non_contiguous_dma(reason="og: one value for each partition and group"):
             nc.sync.dma_start(out=gain[:], in_=og.rearrange("g m o -> m g o"))
-        load_base(0)
-        load("dy1", half(dy, 1))
-        load_base(1)
-        side = nc.gpsimd
+        nc.sync.dma_start(out=value("base", 0, None), in_=columns(base, 0).rearrange("g m c -> m g c"))
+        load("dy1", columns(dy, 1))
+        nc.sync.dma_start(out=value("base", 1, None), in_=columns(base, 1).rearrange("g m c -> m g c"))
 
-        def each_group(f):
-            for g in range(G):
-                f(g)
-
-        def gain_of(g):
-            return gain[:, g, :]
-
-        interleave("x0", "vector")
-        interleave("w1", "vector")
-        interleave("w3", "scalar")
+        round_on_vector("x0")
+        round_on_vector("w1")
+        round_on_scalar("w3", 0, M)
         quantize("x0")
         quantize("w1")
         product("z1", "w1", "x", 0)
-        interleave("w2", "vector")
+        round_on_vector("w2")
         quantize("w3")
         quantize("w2")
         product("z3", "w3", "x", 0)
         product("z2", "w2", "x", 0)
-        each_group(lambda g: act("z1s", "z1", 0, g, ACT.Copy))
-        each_group(lambda g: act("T", "z3", 0, g, ACT.Tanh))
-        act("Tm", "T", 0, None, ACT.Square, bias=-0.5)
-        interleave("dx0", "vector")
+        unary_each("z1_sb", ACT.Copy, "z1", 0)
+        unary_each("T", ACT.Tanh, "z3", 0)
+        unary("T_shift_sq", ACT.Square, "T", 0, bias=-0.5)
+
+        round_on_vector("dx0")
         quantize("dx0")
-        each_group(lambda g: tt("m", "z1s", ALU.mult, "z2", 0, g))
-        each_group(lambda g: tt("p", "m", ALU.add, "z3", 0, g))
+        binary_each("z1_z2", "z1_sb", MULT, "z2", 0)
+        binary_each("gate", "z1_z2", ADD, "z3", 0)
         product("tz2", "w2", "dx", 0)
         product("tz1", "w1", "dx", 0)
         product("tz3", "w3", "dx", 0)
-        each_group(lambda g: act("z2s", "z2", 0, g, ACT.Copy))
-        interleave("x1", "scalar")
-        act("h", "p", 0, None, ACT.Tanh, scale=0.5)
-        act("TT", "T", 0, None, ACT.Square, scale=0.5)
-        act("hh", "h", 0, None, ACT.Square, scale=0.5)
-        interleave("dx1", "scalar")
-        interleave("dy0", "scalar")
-        interleave("wo", "vector")
-        tt("a12", "zs", ALU.mult, "tz21", 0, 0)
+        unary_each("z2_sb", ACT.Copy, "z2", 0)
+        round_on_scalar("x1", 0, HALF)
+        unary("H", ACT.Tanh, "gate", 0, scale=0.5)
+        unary("T_sq", ACT.Square, "T", 0, scale=0.5)
+        unary("H_sq", ACT.Square, "H", 0, scale=0.5)
+        round_on_scalar("dx1", 0, HALF)
+        round_on_vector("wo")
+        binary("cross", "z1z2", MULT, "tz2tz1", 0, 0)
         quantize("wo")
-        tt("a3", "a1", ALU.add, "tz3", 0, 0)
-        tt("A", "a3", ALU.add, "a2", 0, 0, side)
-        tt("a1", "z1s", ALU.mult, "tz2", 0, 1)
-        tt("a2", "z2s", ALU.mult, "tz1", 0, 1)
-        tt("a3", "a1", ALU.add, "tz3", 0, 1)
-        stt("Y", "h", ALU.add, 1.0, ALU.mult, "T", 0)
+        binary("cross", "z1z2", MULT, "tz2tz1", 0, 1)
+        binary_each("z1_tz2_tz3", "z1_tz2", ADD, "tz3", 0)
+
+        fused("Y", "H", ADD, 1.0, MULT, "T", 0)
         quantize("x1")
         product("z1", "w1", "x", 1)
         product("z3", "w3", "x", 1)
         product("z2", "w2", "x", 1)
-        stt("nv", "Tm", ALU.add, -1.25, ALU.add, "Y", 0)
-        stt("nk", "hh", ALU.add, -0.25, ALU.add, "Y", 0)
-        tt("A", "a3", ALU.add, "a2", 0, 1)
+        factors(0)
         quantize("dx1")
         product("tz2", "w2", "dx", 1)
         product("tz1", "w1", "dx", 1)
-        stt("F12", "sq", ALU.add, -0.25, ALU.mult, "nvk", 0)
-        quantize("dy0")
+        fused("F", "squares", ADD, -0.25, MULT, "VK", 0)
         for g in range(G):
-            act("z1s", "z1", 1, g, ACT.Copy)
-            act("T", "z3", 1, g, ACT.Tanh)
-        each_group(lambda g: stt("tF", "F2", ALU.mult, 4.0, ALU.mult, "tz3", 0, g))
-        tt("AF", "A", ALU.mult, "F1", 0, None, side)
-        tt("E", "AF", ALU.add, "tF", 0, None, side)
+            unary("z1_sb", ACT.Copy, "z1", 1, g)
+            unary("T", ACT.Tanh, "z3", 1, g)
+
+        round_on_scalar("dy0", 0, HALF // 2)
+        binary_each("z1_z2", "z1_sb", MULT, "z2", 1)
+        tz3_term(0)
+        binary("A_F1", "A", MULT, "F1", 0, engine=nc.gpsimd)
+        binary("E", "A_F1", ADD, "tz3_F2", 0, engine=nc.gpsimd)
         product("tz3", "w3", "dx", 1)
-        each_group(lambda g: tt("m", "z1s", ALU.mult, "z2", 1, g))
-        each_group(lambda g: tt("p", "m", ALU.add, "z3", 1, g))
-        each_group(lambda g: act("z2s", "z2", 1, g, ACT.Copy))
+        binary_each("gate", "z1_z2", ADD, "z3", 1)
+        unary_each("z2_sb", ACT.Copy, "z2", 1)
+        unary("T_shift_sq", ACT.Square, "T", 1, bias=-0.5)
+        unary("H", ACT.Tanh, "gate", 1, scale=0.5)
+        round_on_scalar("dy0", HALF // 2, HALF)
+        unary("squares", ACT.Square, "HT", 1, scale=0.5)
+        round_on_scalar("dy1", 0, HALF)
+        binary_each("cross", "z1z2", MULT, "tz2tz1", 1)
+        binary_each("z1_tz2_tz3", "z1_tz2", ADD, "tz3", 1)
+
+        fused("Y", "H", ADD, 1.0, MULT, "T", 1)
+        quantize("dy0")
         product("c0", "wo", "dy", 0)
-        act("h", "p", 1, None, ACT.Tanh, scale=0.5)
-        act("Tm", "T", 1, None, ACT.Square, bias=-0.5)
-        act("sq", "hT", 1, None, ACT.Square, scale=0.5)
-        interleave("dy1", "scalar")
-        each_group(lambda g: tt("a12", "zs", ALU.mult, "tz21", 1, g))
-        tt("a3", "a1", ALU.add, "tz3", 1, 0)
-        tt("A", "a3", ALU.add, "a2", 1, 0, side)
-        tt("a3", "a1", ALU.add, "tz3", 1, 1)
-        each_group(lambda g: stt("cE", "E", ALU.mult, gain_of(g), ALU.mult, "c0", 0, g))
-        stt("Y", "h", ALU.add, 1.0, ALU.mult, "T", 1)
-        tt("A", "a3", ALU.add, "a2", 1, 1)
-        stt("nv", "Tm", ALU.add, -1.25, ALU.add, "Y", 1)
-        stt("nk", "hh", ALU.add, -0.25, ALU.add, "Y", 1)
-        tt("res", "cE", ALU.add, "base", 0)
-        nc.sync.dma_start(out=half(out, 0).rearrange("g m c -> m g c"), in_=operand("res", 0, None))
-        stt("F12", "sq", ALU.add, -0.25, ALU.mult, "nvk", 1)
+        factors(1)
+        fused("F", "squares", ADD, -0.25, MULT, "VK", 1)
         quantize("dy1")
         product("c0", "wo", "dy", 1)
-        tt("AF", "A", ALU.mult, "F1", 1)
-        each_group(lambda g: stt("tF", "F2", ALU.mult, 4.0, ALU.mult, "tz3", 1, g))
-        each_group(lambda g: tt("E", "AF", ALU.add, "tF", 1, g))
-        each_group(lambda g: stt("cE", "E", ALU.mult, gain_of(g), ALU.mult, "c0", 1, g))
+
+        binary("A_F1", "A", MULT, "F1", 1, engine=nc.gpsimd)
+        upstream_term(0)
+        tz3_term(1)
+        binary("result", "og_c0_E", ADD, "base", 0)
+        nc.sync.dma_start(out=columns(out, 0).rearrange("g m c -> m g c"), in_=value("result", 0, None))
+
+        binary_each("E", "A_F1", ADD, "tz3_F2", 1)
+        upstream_term(1)
         for g in range(G):
-            tt("res", "cE", ALU.add, "base", 1, g)
-            nc.sync.dma_start(out=half(out, 1)[g], in_=operand("res", 1, g))
+            binary("result", "og_c0_E", ADD, "base", 1, g)
+            nc.sync.dma_start(out=columns(out, 1)[g], in_=value("result", 1, g))

@@ -19,7 +19,7 @@ PACK = 4
 ROWS = D // PACK
 HALF = N // 2
 MM_N = 128
-RUN = 4
+RUN = 2
 
 PLACE = {"z1": (0, 0), "z3": (0, 1), "z2": (1, 0), "c0": (1, 1), "tz2": (2, 0), "tz1": (2, 1), "tz3": (3, 0)}
 MOVED = {("z3", 0): (3, 1), ("c0", 1): (2, 0)}

from contextlib import ExitStack

import concourse.mybir as mybir

G, D, M, N = 2, 256, 128, 512
FLOPS = 7 * 2 * G * D * M * N

F32 = mybir.dt.float32
BF16 = mybir.dt.bfloat16
U32 = mybir.dt.uint32
U8 = mybir.dt.uint8
FP8X4 = mybir.dt.float8_e4m3fn_x4
ACT = mybir.ActivationFunctionType
ADD = mybir.AluOpType.add
MULT = mybir.AluOpType.mult

P = 128
PACK = 4
ROWS = D // PACK
HALF = N // 2
MM_N = 128
RUN = 2

PLACE = {"z1": (0, 0), "z3": (0, 1), "z2": (1, 0), "c0": (1, 1), "tz2": (2, 0), "tz1": (2, 1), "tz3": (3, 0)}
MOVED = {("z3", 0): (3, 1), ("c0", 1): (2, 0)}

GROUP_PAIRS = {"z1z2": ("z1_sb", "z2_sb"), "cross": ("z1_tz2", "z2_tz1")}
WIDE_PAIRS = {"HT": ("H", "T"), "squares": ("H_sq", "T_sq"), "VK": ("V", "K"), "F": ("F1", "F2")}


def tile_rows_hvbilinsig_kernel(tc, x, w1, w2, w3, wo, dy, dx, og, base, out):
    nc = tc.nc

    with ExitStack() as ctx:
        sb = ctx.enter_context(tc.tile_pool(name="sb", bufs=1))
        ps = ctx.enter_context(tc.psum_pool(name="ps", bufs=1))
        ctx.enter_context(tc.manual_schedule())

        raw, rounded, codes, scales = {}, {}, {}, {}

        def columns(tensor, half):
            return tensor[:, :, half * HALF : (half + 1) * HALF]

        def load(name, src):
            width = src.shape[2]
            raw[name] = sb.tile([P, PACK, width], F32, name="raw_" + name)
            rounded[name] = sb.tile([P, width * PACK], BF16, name="rounded_" + name, align_bytes=64)
            nc.sync.dma_start(out=raw[name][:], in_=src.rearrange("g (p j) c -> (g p) j c", j=PACK))

        def rounding_views(name, c0, c1):
            dst = rounded[name][:, PACK * c0 : PACK * c1].rearrange("p (c i j) -> p c j i", i=RUN, j=PACK)
            src = raw[name][:, :, c0:c1].rearrange("p j (c i) -> p c j i", i=RUN)
            return dst, src

        def round_on_vector(name):
            dst, src = rounding_views(name, 0, raw[name].shape[2])
            nc.vector.tensor_copy(out=dst, in_=src)

        def round_on_scalar(name, c0, c1):
            dst, src = rounding_views(name, c0, c1)
            nc.scalar.activation(out=dst, in_=src, func=ACT.Copy)

        def quantize(name):
            width = raw[name].shape[2]
            codes[name] = sb.tile([P, width], U32, name="codes_" + name, align_bytes=64)
            scales[name] = sb.tile([P, width], U8, name="scales_" + name, align_bytes=64)
            nc.vector.quantize_mx(out=codes[name][:].bitcast(FP8X4), scales=scales[name][:], in_=rounded[name][:])

        banks = [[ps.tile([P, 2, HALF], F32, name="bank_%d_%d" % (g, b)) for b in range(4)] for g in range(G)]

        def sums(name, half, g):
            bank, side = MOVED.get((name, half), PLACE[name])
            return banks[g][bank][:, side, :]

        def product(name, weights, source, half):
            moving = "%s%d" % (source, half)
            for n0 in range(0, HALF, MM_N):
                cols = slice(n0, n0 + MM_N)
                for g in range(G):
                    rows = slice(ROWS * g, ROWS * (g + 1))
                    nc.tensor.matmul_mx(
                        out=sums(name, half, g)[:, cols],
                        lhsT=codes[weights][rows, :].bitcast(FP8X4),
                        lhsT_scale=scales[weights][rows, :],
                        rhs=codes[moving][rows, cols].bitcast(FP8X4),
                        rhs_scale=scales[moving][rows, cols],
                        start=True,
                        stop=True,
                    )

        tiles = {}

        def tile_of(name, half, shape):
            if (name, half) not in tiles:
                tiles[(name, half)] = sb.tile(shape, F32, name="%s_%d" % (name, half))
            return tiles[(name, half)]

        def value(name, half, g):
            group = slice(None) if g is None else g
            if name in PLACE:
                return sums(name, half, g)
            if name == "tz2tz1":
                return banks[g][PLACE["tz2"][0]][:].rearrange("p s c -> p (s c)")
            if name in GROUP_PAIRS:
                return tile_of(name, half, [P, G, 2, HALF])[:, g, :, :].rearrange("p s c -> p (s c)")
            if name in WIDE_PAIRS:
                return tile_of(name, half, [P, 2, G, HALF])[:].rearrange("p s g c -> p (s g c)")
            for pair, members in GROUP_PAIRS.items():
                if name in members:
                    return tile_of(pair, half, [P, G, 2, HALF])[:, group, members.index(name), :]
            for pair, members in WIDE_PAIRS.items():
                if name in members:
                    return tile_of(pair, half, [P, 2, G, HALF])[:, members.index(name), group, :]
            return tile_of(name, half, [P, G, HALF])[:, group, :]

        def unary(dst, func, src, half, g=None, scale=1.0, bias=0.0):
            nc.scalar.activation(out=value(dst, half, g), in_=value(src, half, g), func=func, scale=scale, bias=bias)

        def binary(dst, a, op, b, half, g=None, engine=nc.vector):
            engine.tensor_tensor(out=value(dst, half, g), in0=value(a, half, g), in1=value(b, half, g), op=op)

        def fused(dst, a, op0, scalar, op1, b, half, g=None):
            nc.vector.scalar_tensor_tensor(
                out=value(dst, half, g),
                in0=value(a, half, g),
                scalar=scalar,
                in1=value(b, half, g),
                op0=op0,
                op1=op1,
            )

        def unary_each(dst, func, src, half):
            for g in range(G):
                unary(dst, func, src, half, g)

        def binary_each(dst, a, op, b, half):
            for g in range(G):
                binary(dst, a, op, b, half, g)

        def tz3_term(half):
            for g in range(G):
                fused("tz3_F2", "F2", MULT, 4.0, MULT, "tz3", half, g)

        def upstream_term(half):
            for g in range(G):
                fused("og_c0_E", "E", MULT, gain[:, g, :], MULT, "c0", half, g)

        def factors(half):
            fused("V", "T_shift_sq", ADD, -1.25, ADD, "Y", half)
            fused("K", "H_sq", ADD, -0.25, ADD, "Y", half)
            binary("A", "z1_tz2_tz3", ADD, "z2_tz1", half)

        load("x0", columns(x, 0))
        load("w1", w1)
        load("w3", w3)
        load("w2", w2)
        load("dx0", columns(dx, 0))
        load("wo", wo)
        load("x1", columns(x, 1))
        load("dx1", columns(dx, 1))
        load("dy0", columns(dy, 0))
        gain = sb.tile([P, G, 1], F32, name="gain")
        with nc.allow_non_contiguous_dma(reason="og: one value for each partition and group"):
            nc.sync.dma_start(out=gain[:], in_=og.rearrange("g m o -> m g o"))
        nc.sync.dma_start(out=value("base", 0, None), in_=columns(base, 0).rearrange("g m c -> m g c"))
        load("dy1", columns(dy, 1))
        nc.sync.dma_start(out=value("base", 1, None), in_=columns(base, 1).rearrange("g m c -> m g c"))

        round_on_vector("x0")
        round_on_vector("w1")
        round_on_scalar("w3", 0, M)
        quantize("x0")
        quantize("w1")
        product("z1", "w1", "x", 0)
        round_on_vector("w2")
        quantize("w3")
        quantize("w2")
        product("z3", "w3", "x", 0)
        product("z2", "w2", "x", 0)
        unary_each("z1_sb", ACT.Copy, "z1", 0)
        unary_each("T", ACT.Tanh, "z3", 0)
        unary("T_shift_sq", ACT.Square, "T", 0, bias=-0.5)

        round_on_vector("dx0")
        quantize("dx0")
        binary_each("z1_z2", "z1_sb", MULT, "z2", 0)
        binary_each("gate", "z1_z2", ADD, "z3", 0)
        product("tz2", "w2", "dx", 0)
        product("tz1", "w1", "dx", 0)
        product("tz3", "w3", "dx", 0)
        unary_each("z2_sb", ACT.Copy, "z2", 0)
        round_on_scalar("x1", 0, HALF)
        unary("H", ACT.Tanh, "gate", 0, scale=0.5)
        unary("T_sq", ACT.Square, "T", 0, scale=0.5)
        unary("H_sq", ACT.Square, "H", 0, scale=0.5)
        round_on_scalar("dx1", 0, HALF)
        round_on_vector("wo")
        binary("cross", "z1z2", MULT, "tz2tz1", 0, 0)
        quantize("wo")
        binary("cross", "z1z2", MULT, "tz2tz1", 0, 1)
        binary_each("z1_tz2_tz3", "z1_tz2", ADD, "tz3", 0)

        fused("Y", "H", ADD, 1.0, MULT, "T", 0)
        quantize("x1")
        product("z1", "w1", "x", 1)
        product("z3", "w3", "x", 1)
        product("z2", "w2", "x", 1)
        factors(0)
        quantize("dx1")
        product("tz2", "w2", "dx", 1)
        product("tz1", "w1", "dx", 1)
        fused("F", "squares", ADD, -0.25, MULT, "VK", 0)
        for g in range(G):
            unary("z1_sb", ACT.Copy, "z1", 1, g)
            unary("T", ACT.Tanh, "z3", 1, g)

        round_on_scalar("dy0", 0, HALF // 2)
        binary_each("z1_z2", "z1_sb", MULT, "z2", 1)
        tz3_term(0)
        binary("A_F1", "A", MULT, "F1", 0, engine=nc.gpsimd)
        binary("E", "A_F1", ADD, "tz3_F2", 0, engine=nc.gpsimd)
        product("tz3", "w3", "dx", 1)
        binary_each("gate", "z1_z2", ADD, "z3", 1)
        unary_each("z2_sb", ACT.Copy, "z2", 1)
        unary("T_shift_sq", ACT.Square, "T", 1, bias=-0.5)
        unary("H", ACT.Tanh, "gate", 1, scale=0.5)
        round_on_scalar("dy0", HALF // 2, HALF)
        unary("squares", ACT.Square, "HT", 1, scale=0.5)
        round_on_scalar("dy1", 0, HALF)
        binary_each("cross", "z1z2", MULT, "tz2tz1", 1)
        binary_each("z1_tz2_tz3", "z1_tz2", ADD, "tz3", 1)

        fused("Y", "H", ADD, 1.0, MULT, "T", 1)
        quantize("dy0")
        product("c0", "wo", "dy", 0)
        factors(1)
        fused("F", "squares", ADD, -0.25, MULT, "VK", 1)
        quantize("dy1")
        product("c0", "wo", "dy", 1)

        binary("A_F1", "A", MULT, "F1", 1, engine=nc.gpsimd)
        upstream_term(0)
        tz3_term(1)
        binary("result", "og_c0_E", ADD, "base", 0)
        nc.sync.dma_start(out=columns(out, 0).rearrange("g m c -> m g c"), in_=value("result", 0, None))

        binary_each("E", "A_F1", ADD, "tz3_F2", 1)
        upstream_term(1)
        for g in range(G):
            binary("result", "og_c0_E", ADD, "base", 1, g)
            nc.sync.dma_start(out=columns(out, 1)[g], in_=value("result", 1, g))
